import numpy as np
import ml_dtypes


def mxq(x, axis, fmt="e4m3"):
    dtype, down = {"e4m3": (ml_dtypes.float8_e4m3fn, 7), "e5m2": (ml_dtypes.float8_e5m2, 14)}[fmt]
    v = np.moveaxis(np.asarray(x, np.float32).astype(ml_dtypes.bfloat16).astype(np.float64), axis, -1)
    blocks = v.reshape(v.shape[:-1] + (-1, 32))
    amax = np.abs(blocks).max(-1, keepdims=True)
    byte = np.maximum(np.where(amax > 0, np.frexp(amax)[1] - 1 + 127, 0) - down, 1)
    scale = np.exp2(byte - 127.0)
    codes = (blocks / scale).astype(np.float32).astype(dtype).astype(np.float64)
    return np.moveaxis((codes * scale).reshape(v.shape), -1, axis)


WIDE = False


def mx_kscale(k):
    if not WIDE:
        return np.ones(k)
    levels = np.array([10, -10, 5, -5, 0])
    if k % 512:
        return np.exp2(np.random.permutation(np.resize(levels, k // 32))).repeat(32)
    a = np.empty((k // 512, 16))
    for p in range(k // 512):
        a[p, :8] = np.random.permutation(np.resize(levels, 8))
        for g in range(8):
            far = levels[np.abs(levels - a[p, g]) >= 10]
            a[p, g + 8] = far[np.random.randint(len(far))]
    return np.exp2(a.ravel()).repeat(32)


def f64(x):
    return np.asarray(x).astype(np.float64)


def striped(idx):
    return np.tile(idx.reshape(-1, 16).T, (8, 1)).astype(np.uint16)


def unstriped(offs):
    return offs[:16].T.reshape(-1).astype(np.int64)


def relu2(v):
    return np.maximum(v, 0.0) ** 2


K, T, E, C, N = 1024, 1280, 6, 128, 512


def by_expert(wq, xq):
    return np.concatenate([wq[e].T @ xq[:, e * C:(e + 1) * C] for e in range(E)], axis=1)


def setup_inputs():
    n = np.random.standard_normal
    s = mx_kscale(K)[:, None]
    return {
        "xT": (n((K, T)) * s).astype(np.float32),
        "w": (n((E + 1, K, N)) / np.sqrt(K) / s[None]).astype(np.float32),
        "b": (0.3 * n((N, E + 1))).astype(np.float32),
        "gate": np.tile(np.random.uniform(0.2, 1.0, E * C), (N, 1)).astype(np.float32),
        "offs": striped(np.random.permutation(T)[:E * C]),
    }


def reference(xT, w, b, gate, offs):
    idx = unstriped(offs)
    wq = mxq(f64(w), 1, "e4m3")
    xs = mxq(f64(xT), 0, "e4m3")
    ys = relu2((wq[E].T @ xs) + f64(b)[:, E:])
    xq = mxq(f64(xT)[:, idx], 0, "e4m3")
    y = by_expert(wq, xq)
    y = relu2(y + np.repeat(f64(b)[:, :E], C, axis=1))
    out = ys
    out[:, idx] += f64(gate) * y
    return out

@@ -1,0 +1,210 @@
+from contextlib import ExitStack
+
+import concourse.mybir as mybir
+
+K, T, E, C, N = 1024, 1280, 6, 128, 512
+SLOTS = E * C
+P = 128
+KP = 512
+PASSES = K // KP
+NT = N // P
+
+FLOPS = 2 * K * N * (SLOTS + T)
+BYTES = 4 * (K * T + (E + 1) * K * N + N * (E + 1) + P * SLOTS + N * T) + 2 * P * SLOTS // 16
+
+F32 = mybir.dt.float32
+BF16 = mybir.dt.bfloat16
+U32 = mybir.dt.uint32
+U16 = mybir.dt.uint16
+U8 = mybir.dt.uint8
+X4 = mybir.dt.float8_e4m3fn_x4
+ACT = mybir.ActivationFunctionType
+ALU = mybir.AluOpType
+
+S_SHARE = 432
+X_VECTOR = (640, 800, 0, 0)
+GROUPS = [(0, 256), (256, 512), (512, 768)]
+LAG = 3
+
+
+def tile_moe_shr_lin_relu2_kernel(tc, xT, w, b, gate, offs, out):
+    nc = tc.nc
+    with ExitStack() as ctx:
+        keep = ctx.enter_context(tc.tile_pool(name="keep", bufs=1))
+        raws = ctx.enter_context(tc.tile_pool(name="raws", bufs=7))
+        wbfp = ctx.enter_context(tc.tile_pool(name="wbfp", bufs=3))
+        wqp = ctx.enter_context(tc.tile_pool(name="wqp", bufs=3))
+        xst = ctx.enter_context(tc.tile_pool(name="xst", bufs=2))
+        xst1 = ctx.enter_context(tc.tile_pool(name="xst1", bufs=1))
+        rp = ctx.enter_context(tc.tile_pool(name="rp", bufs=3))
+        psum = ctx.enter_context(tc.psum_pool(name="psum", bufs=8))
+
+        offsets = keep.tile([P, SLOTS // 16], U16, name="offsets")
+        nc.sync.dma_start(offsets[:], offs)
+
+        xr = {}
+        for c in range(PASSES):
+            rows = xT[c * KP : (c + 1) * KP, :].rearrange("(p u e) t -> p u e t", u=2, e=2)
+            for u in range(2):
+                raw = raws.tile([P, 2, T], F32, tag="raw", name=f"x{c}{u}")
+                cuts = (0, T // 2, T) if (c, u) == (0, 0) else (0, T)
+                for lo, hi in zip(cuts[:-1], cuts[1:]):
+                    nc.sync.dma_start(raw[:, :, lo:hi], rows[:, u, :, lo:hi])
+                xr[c, u] = raw
+
+        bias = keep.tile([P, NT, E + 1], F32, name="bias")
+        nc.sync.dma_start(bias[:], b.rearrange("(n p) e -> p n e", p=P))
+
+        wr = {}
+
+        def load_w(e):
+            for c in range(PASSES):
+                raw = raws.tile([P, 4, N], F32, tag="raw", name=f"w{e}{c}")
+                nc.sync.dma_start(raw[:], w[e, c * KP : (c + 1) * KP, :].rearrange("(p j) n -> p j n", j=4))
+                wr[e, c] = raw
+
+        load_w(0)
+        load_w(1)
+        gsb = keep.tile([P, SLOTS], F32, name="gsb")
+        nc.sync.dma_start(gsb[:], gate[0:P, :])
+
+        z = []
+        for n in range(NT):
+            zt = keep.tile([P, T], F32, name=f"z{n}")
+            nc.gpsimd.memset(zt[:], 0.0)
+            z.append(zt)
+
+        xps, sq, ss = [], [], []
+        for c in range(PASSES):
+            xp = xst.tile([P, 2, T, 2], BF16, tag="xp", name=f"xp{c}", align_bytes=64)
+            gw = xst1.tile([P, 2, SLOTS, 2], BF16, tag="gw", name=f"gw{c}", align_bytes=64)
+            for u in range(2):
+                cut = T - X_VECTOR[2 * c + u]
+                nc.scalar.copy(xp[:, u, 0:cut, :], xr[c, u][:, :, 0:cut].rearrange("p e t -> p t e"))
+                if cut < T:
+                    nc.vector.tensor_copy(xp[:, u, cut:T, :], xr[c, u][:, :, cut:T].rearrange("p e t -> p t e"))
+                nc.vector.tensor_copy(
+                    gw[:, u, :, :].rearrange("p j e -> p (j e)").bitcast(U32),
+                    xp[:, u, :, :].rearrange("p t e -> p (t e)").bitcast(U32).indirect(offsets[:]),
+                )
+            gi = xst1.tile([P, SLOTS, 2, 2], BF16, tag="gi", name=f"gi{c}", align_bytes=64)
+            nc.vector.tensor_copy(gi[:], gw[:].rearrange("p u j e -> p j u e"))
+            scodes = keep.tile([P, SLOTS], U32, name=f"scodes{c}", align_bytes=64)
+            sscale = keep.tile([P, SLOTS], U8, name=f"sscale{c}", align_bytes=64)
+            flat = gi[:].rearrange("p j u e -> p (j u e)")
+            for lo, hi in ((0, 512), (512, 768)):
+                nc.vector.quantize_mx(scodes[:, lo:hi].bitcast(X4), sscale[:, lo:hi], flat[:, 4 * lo : 4 * hi])
+            xps.append(xp)
+            sq.append(scodes)
+            ss.append(sscale)
+
+        load_w(2)
+        load_w(3)
+
+        def quantised(e, n0, n1):
+            width = n1 - n0
+            wb = wbfp.tile([P, PASSES, width, 4], BF16, tag="wb", name=f"wb{e}_{n0}", align_bytes=64)
+            for c in range(PASSES):
+                cut = S_SHARE * width // N
+                dst = wb[:, c, :, :].rearrange("p (k i) t -> p k t i", i=4)
+                src = wr[e, c][:, :, n0:n1].rearrange("p t (k i) -> p k t i", i=4)
+                k = cut // 4
+                nc.scalar.copy(dst[:, 0:k, :, :], src[:, 0:k, :, :])
+                if cut < width:
+                    nc.vector.tensor_copy(dst[:, k:, :, :], src[:, k:, :, :])
+            q = wqp.tile([P, PASSES * width], U32, tag="wq", name=f"wq{e}_{n0}", align_bytes=64)
+            s = wqp.tile([P, PASSES * width], U8, tag="ws", name=f"ws{e}_{n0}", align_bytes=64)
+            nc.vector.quantize_mx(q[:].bitcast(X4), s[:], wb[:].rearrange("p c n t -> p (c n t)"))
+            return q, s, width
+
+        def product(ps, weights, m, codes, scales, lo, hi):
+            q, s, width = weights
+            for c in range(PASSES):
+                cols = slice(c * width + m * P, c * width + (m + 1) * P)
+                nc.tensor.matmul_mx(
+                    out=ps,
+                    lhsT=q[:, cols].bitcast(X4),
+                    lhsT_scale=s[:, cols],
+                    rhs=codes[c][:, lo:hi].bitcast(X4),
+                    rhs_scale=scales[c][:, lo:hi],
+                    start=(c == 0),
+                    stop=(c == PASSES - 1),
+                )
+
+        r = {}
+        pending = []
+
+        def scatter(g):
+            lo, hi = GROUPS[g]
+            for n in range(NT):
+                nc.vector.tensor_tensor(
+                    z[n][:].indirect(offsets[:, lo // 16 : hi // 16]), r[g][:, n, :], gsb[:, lo:hi], ALU.mult
+                )
+
+        def routed(e):
+            weights = quantised(e, 0, N)
+            ps = psum.tile([P, NT, C], F32, tag="ps", name=f"pse{e}")
+            for n in range(NT):
+                product(ps[:, n, :], weights, n, sq, ss, e * C, (e + 1) * C)
+            for g, (lo, hi) in enumerate(GROUPS):
+                a, z1 = max(lo, e * C), min(hi, (e + 1) * C)
+                if a >= z1:
+                    continue
+                if g not in r:
+                    r[g] = rp.tile([P, NT, hi - lo], F32, tag="r", name=f"r{g}")
+                for n in range(NT):
+                    nc.scalar.activation(
+                        r[g][:, n, a - lo : z1 - lo],
+                        ps[:, n, a - e * C : z1 - e * C],
+                        ACT.Relu,
+                        bias=bias[:, n, e : e + 1],
+                    )
+                nc.scalar.activation(r[g][:, :, a - lo : z1 - lo], r[g][:, :, a - lo : z1 - lo], ACT.Square)
+                if z1 == hi:
+                    pending.append((e + LAG, g))
+
+        def flush(step):
+            while pending and pending[0][0] <= step:
+                scatter(pending[0][1])
+                pending.remove(pending[0])
+
+        for e in range(E):
+            if e + 4 <= E:
+                load_w(e + 4)
+            routed(e)
+            flush(e)
+
+        xq, xs = [], []
+        for c in range(PASSES):
+            xi = xst1.tile([P, T, 2, 2], BF16, tag="xi", name=f"xi{c}", align_bytes=64)
+            nc.vector.tensor_copy(xi[:], xps[c][:].rearrange("p u t e -> p t u e"))
+            xcodes = keep.tile([P, T], U32, name=f"xcodes{c}", align_bytes=64)
+            xscale = keep.tile([P, T], U8, name=f"xscale{c}", align_bytes=64)
+            flat = xi[:].rearrange("p j u e -> p (j u e)")
+            for lo, hi in ((0, 1024), (1024, 1280)):
+                nc.vector.quantize_mx(xcodes[:, lo:hi].bitcast(X4), xscale[:, lo:hi], flat[:, 4 * lo : 4 * hi])
+            xq.append(xcodes)
+            xs.append(xscale)
+
+        chunks = ((0, 512), (512, 1024), (1024, 1280))
+        ys = []
+        for h in range(2):
+            weights = quantised(E, h * N // 2, (h + 1) * N // 2)
+            for m in range(NT // 2):
+                n = h * (NT // 2) + m
+                yt = keep.tile([P, T], F32, name=f"ys{n}")
+                for lo, hi in chunks:
+                    ps = psum.tile([P, 512], F32, tag="ps", name=f"pss{n}_{lo}")
+                    product(ps[:, 0 : hi - lo], weights, m, xq, xs, lo, hi)
+                    nc.scalar.activation(yt[:, lo:hi], ps[:, 0 : hi - lo], ACT.Relu, bias=bias[:, n, E : E + 1])
+                    if n == NT - 1:
+                        nc.scalar.activation(yt[:, lo:hi], yt[:, lo:hi], ACT.Square)
+                if n < NT - 1:
+                    nc.scalar.activation(yt[:], yt[:], ACT.Square)
+                ys.append(yt)
+            flush(E + h)
+        flush(E + LAG)
+        for n in range(NT):
+            for lo, hi in chunks if n == NT - 1 else ((0, T),):
+                nc.vector.tensor_tensor(ys[n][:, lo:hi], ys[n][:, lo:hi], z[n][:, lo:hi], ALU.add)
+                nc.sync.dma_start(out[n * P : (n + 1) * P, lo:hi], ys[n][:, lo:hi])

@@ -15,16 +15,18 @@ BYTES = 4 * (K * T + (E + 1) * K * N + N * (E + 1) + P * SLOTS + N * T) + 2 * P 
 F32 = mybir.dt.float32
 BF16 = mybir.dt.bfloat16
 U32 = mybir.dt.uint32
+I32 = mybir.dt.int32
 U16 = mybir.dt.uint16
 U8 = mybir.dt.uint8
 X4 = mybir.dt.float8_e4m3fn_x4
 ACT = mybir.ActivationFunctionType
 ALU = mybir.AluOpType
 
-S_SHARE = 432
+S_SHARE = 464
+G_SHARE = 0
 X_VECTOR = (640, 800, 0, 0)
-GROUPS = [(0, 256), (256, 512), (512, 768)]
-LAG = 3
+FILL = {1: [("x", 0)], 2: [("x", 1)], 3: [(0, 0), (0, 1)], 4: [(0, 2), (0, 3)], 5: [(1, 0), (1, 1)], 6: [(1, 2), (1, 3)], 7: [(2, 0)]}
+POST = {7: [(2, 1), (2, 2)], 8: [(2, 3)]}
 
 
 def tile_moe_shr_lin_relu2_kernel(tc, xT, w, b, gate, offs, out):
@@ -88,7 +90,10 @@ def tile_moe_shr_lin_relu2_kernel(tc, xT, w, b, gate, offs, out):
                     xp[:, u, :, :].rearrange("p t e -> p (t e)").bitcast(U32).indirect(offsets[:]),
                 )
             gi = xst1.tile([P, SLOTS, 2, 2], BF16, tag="gi", name=f"gi{c}", align_bytes=64)
-            nc.vector.tensor_copy(gi[:], gw[:].rearrange("p u j e -> p j u e"))
+            nc.vector.tensor_copy(
+                gi[:].rearrange("p j u e -> p (j u e)").bitcast(I32).rearrange("p (j u) -> p j u", u=2),
+                gw[:].rearrange("p u j e -> p (u j e)").bitcast(I32).rearrange("p (u j) -> p j u", u=2),
+            )
             scodes = keep.tile([P, SLOTS], U32, name=f"scodes{c}", align_bytes=64)
             sscale = keep.tile([P, SLOTS], U8, name=f"sscale{c}", align_bytes=64)
             flat = gi[:].rearrange("p j u e -> p (j u e)")
@@ -101,24 +106,53 @@ def tile_moe_shr_lin_relu2_kernel(tc, xT, w, b, gate, offs, out):
         load_w(2)
         load_w(3)
 
-        def quantised(e, n0, n1):
+        xq, xs = [], []
+
+        def quantise_tokens(c):
+            xi = xst1.tile([P, T, 2, 2], BF16, tag="xi", name=f"xi{c}", align_bytes=64)
+            nc.vector.tensor_copy(
+                xi[:].rearrange("p t u e -> p (t u e)").bitcast(I32).rearrange("p (t u) -> p t u", u=2),
+                xps[c][:].rearrange("p u t e -> p (u t e)").bitcast(I32).rearrange("p (u t) -> p t u", u=2),
+            )
+            xcodes = keep.tile([P, T], U32, name=f"xcodes{c}", align_bytes=64)
+            xscale = keep.tile([P, T], U8, name=f"xscale{c}", align_bytes=64)
+            flat = xi[:].rearrange("p j u e -> p (j u e)")
+            for lo, hi in ((0, 1024), (1024, 1280)):
+                nc.vector.quantize_mx(xcodes[:, lo:hi].bitcast(X4), xscale[:, lo:hi], flat[:, 4 * lo : 4 * hi])
+            xq.append(xcodes)
+            xs.append(xscale)
+
+        def columns(i):
+            return (i, 0, N) if i < E else (E, (i - E) * N // 2, (i - E + 1) * N // 2)
+
+        cast_tiles, weights, banks = {}, {}, {}
+
+        def cast(i):
+            e, n0, n1 = columns(i)
             width = n1 - n0
-            wb = wbfp.tile([P, PASSES, width, 4], BF16, tag="wb", name=f"wb{e}_{n0}", align_bytes=64)
+            wb = wbfp.tile([P, PASSES, width, 4], BF16, tag="wb", name=f"wb{i}", align_bytes=64)
+            k1 = S_SHARE * width // N // 4
+            k2 = k1 + G_SHARE * width // N // 4
             for c in range(PASSES):
-                cut = S_SHARE * width // N
                 dst = wb[:, c, :, :].rearrange("p (k i) t -> p k t i", i=4)
                 src = wr[e, c][:, :, n0:n1].rearrange("p t (k i) -> p k t i", i=4)
-                k = cut // 4
-                nc.scalar.copy(dst[:, 0:k, :, :], src[:, 0:k, :, :])
-                if cut < width:
-                    nc.vector.tensor_copy(dst[:, k:, :, :], src[:, k:, :, :])
-            q = wqp.tile([P, PASSES * width], U32, tag="wq", name=f"wq{e}_{n0}", align_bytes=64)
-            s = wqp.tile([P, PASSES * width], U8, tag="ws", name=f"ws{e}_{n0}", align_bytes=64)
-            nc.vector.quantize_mx(q[:].bitcast(X4), s[:], wb[:].rearrange("p c n t -> p (c n t)"))
-            return q, s, width
+                nc.scalar.copy(dst[:, 0:k1, :, :], src[:, 0:k1, :, :])
+                if k1 < k2:
+                    nc.gpsimd.tensor_scalar(dst[:, k1:k2, :, :], src[:, k1:k2, :, :], 1.0, 0.0, op0=ALU.mult, op1=ALU.add)
+                if k2 < width // 4:
+                    nc.vector.tensor_copy(dst[:, k2:, :, :], src[:, k2:, :, :])
+            cast_tiles[i] = wb
 
-        def product(ps, weights, m, codes, scales, lo, hi):
-            q, s, width = weights
+        def quantise(i):
+            e, n0, n1 = columns(i)
+            width = n1 - n0
+            q = wqp.tile([P, PASSES * width], U32, tag="wq", name=f"wq{i}", align_bytes=64)
+            s = wqp.tile([P, PASSES * width], U8, tag="ws", name=f"ws{i}", align_bytes=64)
+            nc.vector.quantize_mx(q[:].bitcast(X4), s[:], cast_tiles[i][:].rearrange("p c n t -> p (c n t)"))
+            weights[i] = q, s, width
+
+        def product(ps, i, m, codes, scales, lo, hi):
+            q, s, width = weights[i]
             for c in range(PASSES):
                 cols = slice(c * width + m * P, c * width + (m + 1) * P)
                 nc.tensor.matmul_mx(
@@ -131,79 +165,68 @@ def tile_moe_shr_lin_relu2_kernel(tc, xT, w, b, gate, offs, out):
                     stop=(c == PASSES - 1),
                 )
 
-        r = {}
-        pending = []
-
-        def scatter(g):
-            lo, hi = GROUPS[g]
-            for n in range(NT):
-                nc.vector.tensor_tensor(
-                    z[n][:].indirect(offsets[:, lo // 16 : hi // 16]), r[g][:, n, :], gsb[:, lo:hi], ALU.mult
-                )
-
-        def routed(e):
-            weights = quantised(e, 0, N)
-            ps = psum.tile([P, NT, C], F32, tag="ps", name=f"pse{e}")
-            for n in range(NT):
-                product(ps[:, n, :], weights, n, sq, ss, e * C, (e + 1) * C)
-            for g, (lo, hi) in enumerate(GROUPS):
-                a, z1 = max(lo, e * C), min(hi, (e + 1) * C)
-                if a >= z1:
-                    continue
-                if g not in r:
-                    r[g] = rp.tile([P, NT, hi - lo], F32, tag="r", name=f"r{g}")
-                for n in range(NT):
-                    nc.scalar.activation(
-                        r[g][:, n, a - lo : z1 - lo],
-                        ps[:, n, a - e * C : z1 - e * C],
-                        ACT.Relu,
-                        bias=bias[:, n, e : e + 1],
-                    )
-                nc.scalar.activation(r[g][:, :, a - lo : z1 - lo], r[g][:, :, a - lo : z1 - lo], ACT.Square)
-                if z1 == hi:
-                    pending.append((e + LAG, g))
-
-        def flush(step):
-            while pending and pending[0][0] <= step:
-                scatter(pending[0][1])
-                pending.remove(pending[0])
-
-        for e in range(E):
-            if e + 4 <= E:
-                load_w(e + 4)
-            routed(e)
-            flush(e)
-
-        xq, xs = [], []
-        for c in range(PASSES):
-            xi = xst1.tile([P, T, 2, 2], BF16, tag="xi", name=f"xi{c}", align_bytes=64)
-            nc.vector.tensor_copy(xi[:], xps[c][:].rearrange("p u t e -> p t u e"))
-            xcodes = keep.tile([P, T], U32, name=f"xcodes{c}", align_bytes=64)
-            xscale = keep.tile([P, T], U8, name=f"xscale{c}", align_bytes=64)
-            flat = xi[:].rearrange("p j u e -> p (j u e)")
-            for lo, hi in ((0, 1024), (1024, 1280)):
-                nc.vector.quantize_mx(xcodes[:, lo:hi].bitcast(X4), xscale[:, lo:hi], flat[:, 4 * lo : 4 * hi])
-            xq.append(xcodes)
-            xs.append(xscale)
-
         chunks = ((0, 512), (512, 1024), (1024, 1280))
-        ys = []
-        for h in range(2):
-            weights = quantised(E, h * N // 2, (h + 1) * N // 2)
+        r, ys = {}, {}
+
+        def multiply(i):
+            if i < E:
+                ps = psum.tile([P, NT, C], F32, tag="ps", name=f"ps{i}")
+                for n in range(NT):
+                    product(ps[:, n, :], i, n, sq, ss, i * C, (i + 1) * C)
+                banks[i] = ps
+                return
             for m in range(NT // 2):
-                n = h * (NT // 2) + m
+                n = (i - E) * (NT // 2) + m
+                for lo, hi in chunks:
+                    ps = psum.tile([P, 512], F32, tag="ps", name=f"ps{i}_{n}_{lo}")
+                    product(ps[:, 0 : hi - lo], i, m, xq, xs, lo, hi)
+                    banks[n, lo] = ps
+
+        def activate(i):
+            if i < E:
+                g, h = i // 2, i % 2
+                if h == 0:
+                    r[g] = rp.tile([P, NT, 2 * C], F32, tag="r", name=f"r{g}")
+                half = r[g][:, :, h * C : (h + 1) * C]
+                for n in range(NT):
+                    nc.scalar.activation(half[:, n, :], banks[i][:, n, :], ACT.Relu, bias=bias[:, n, i : i + 1])
+                nc.scalar.activation(half, half, ACT.Square)
+                return
+            for m in range(NT // 2):
+                n = (i - E) * (NT // 2) + m
                 yt = keep.tile([P, T], F32, name=f"ys{n}")
                 for lo, hi in chunks:
-                    ps = psum.tile([P, 512], F32, tag="ps", name=f"pss{n}_{lo}")
-                    product(ps[:, 0 : hi - lo], weights, m, xq, xs, lo, hi)
-                    nc.scalar.activation(yt[:, lo:hi], ps[:, 0 : hi - lo], ACT.Relu, bias=bias[:, n, E : E + 1])
+                    nc.scalar.activation(
+                        yt[:, lo:hi], banks[n, lo][:, 0 : hi - lo], ACT.Relu, bias=bias[:, n, E : E + 1]
+                    )
                     if n == NT - 1:
                         nc.scalar.activation(yt[:, lo:hi], yt[:, lo:hi], ACT.Square)
                 if n < NT - 1:
                     nc.scalar.activation(yt[:], yt[:], ACT.Square)
-                ys.append(yt)
-            flush(E + h)
-        flush(E + LAG)
+                ys[n] = yt
+
+        def fill(items):
+            for g, n in items:
+                if g == "x":
+                    quantise_tokens(n)
+                    continue
+                lo, hi = 2 * g * C, 2 * (g + 1) * C
+                nc.vector.tensor_tensor(
+                    z[n][:].indirect(offsets[:, lo // 16 : hi // 16]), r[g][:, n, :], gsb[:, lo:hi], ALU.mult
+                )
+
+        for i in range(E + 3):
+            if i + 4 <= E:
+                load_w(i + 4)
+            if i < E + 2:
+                cast(i)
+            if i > 0:
+                activate(i - 1)
+            fill(FILL.get(i, ()))
+            if i < E + 2:
+                quantise(i)
+                multiply(i)
+            fill(POST.get(i, ()))
         for n in range(NT):
             for lo, hi in chunks if n == NT - 1 else ((0, T),):
                 nc.vector.tensor_tensor(ys[n][:, lo:hi], ys[n][:, lo:hi], z[n][:, lo:hi], ALU.add)

@@ -10,7 +10,6 @@ PASSES = K // KP
 NT = N // P
 
 FLOPS = 2 * K * N * (SLOTS + T)
-BYTES = 4 * (K * T + (E + 1) * K * N + N * (E + 1) + P * SLOTS + N * T) + 2 * P * SLOTS // 16
 
 F32 = mybir.dt.float32
 BF16 = mybir.dt.bfloat16
@@ -22,22 +21,24 @@ X4 = mybir.dt.float8_e4m3fn_x4
 ACT = mybir.ActivationFunctionType
 ALU = mybir.AluOpType
 
-S_SHARE = 464
-G_SHARE = 0
-X_VECTOR = (640, 800, 0, 0)
-FILL = {1: [("x", 0)], 2: [("x", 1)], 3: [(0, 0), (0, 1)], 4: [(0, 2), (0, 3)], 5: [(1, 0), (1, 1)], 6: [(1, 2), (1, 3)], 7: [(2, 0)]}
-POST = {7: [(2, 1), (2, 2)], 8: [(2, 3)]}
+S_SHARE = ((0, 512), (448, 480), (256, 256), (320, 0), (0, 512), (320, 512), (512, 0), (512, 416))
+EPILOGUE = "SSSSSS"
+VECTOR_SQUARES = ()
+SCALAR_TOKENS = (1, )
+X_VECTOR = (640, 800, 640, 0)
+GATES_AFTER = {(3, 1): [(0, 2)], (4, 0): [(0, 3)], (4, 1): [(0, 0)], (5, 0): [(1, 0), (1, 2), (1, 1), (1, 3)], (6, 0): [(2, 0)], (6, 1): [(0, 1), (2, 1), (2, 3), (2, 2)]}
 
 
 def tile_moe_shr_lin_relu2_kernel(tc, xT, w, b, gate, offs, out):
     nc = tc.nc
     with ExitStack() as ctx:
         keep = ctx.enter_context(tc.tile_pool(name="keep", bufs=1))
-        raws = ctx.enter_context(tc.tile_pool(name="raws", bufs=7))
+        raws = ctx.enter_context(tc.tile_pool(name="raws", bufs=8))
         wbfp = ctx.enter_context(tc.tile_pool(name="wbfp", bufs=3))
         wqp = ctx.enter_context(tc.tile_pool(name="wqp", bufs=3))
         xst = ctx.enter_context(tc.tile_pool(name="xst", bufs=2))
         xst1 = ctx.enter_context(tc.tile_pool(name="xst1", bufs=1))
+        mixp = ctx.enter_context(tc.tile_pool(name="mixp", bufs=1))
         rp = ctx.enter_context(tc.tile_pool(name="rp", bufs=3))
         psum = ctx.enter_context(tc.psum_pool(name="psum", bufs=8))
 
@@ -59,16 +60,31 @@ def tile_moe_shr_lin_relu2_kernel(tc, xT, w, b, gate, offs, out):
 
         wr = {}
 
-        def load_w(e):
-            for c in range(PASSES):
-                raw = raws.tile([P, 4, N], F32, tag="raw", name=f"w{e}{c}")
-                nc.sync.dma_start(raw[:], w[e, c * KP : (c + 1) * KP, :].rearrange("(p j) n -> p j n", j=4))
-                wr[e, c] = raw
+        def load_w(e, c):
+            raw = raws.tile([P, 4, N], F32, tag="raw", name=f"w{e}{c}")
+            nc.sync.dma_start(raw[:], w[e, c * KP : (c + 1) * KP, :].rearrange("(p j) n -> p j n", j=4))
+            wr[e, c] = raw
 
-        load_w(0)
-        load_w(1)
-        gsb = keep.tile([P, SLOTS], F32, name="gsb")
-        nc.sync.dma_start(gsb[:], gate[0:P, :])
+        order = []
+        for e in range(E + 1):
+            for c in range(PASSES):
+                order.append((e, c))
+                order.extend(("gate", piece) for piece in GATES_AFTER.get((e, c), ()))
+        gates = {}
+
+        def load_through(e):
+            while order and (order[0][0] == "gate" or order[0][0] <= e):
+                kind, what = order[0]
+                order.remove(order[0])
+                if kind == "gate":
+                    g, n = what
+                    piece = raws.tile([P, 2 * C], F32, tag="raw", name=f"gate{g}{n}")
+                    nc.sync.dma_start(piece[:], gate[n * P : (n + 1) * P, 2 * g * C : 2 * (g + 1) * C])
+                    gates[g, n] = piece
+                else:
+                    load_w(kind, what)
+
+        load_through(1)
 
         z = []
         for n in range(NT):
@@ -89,7 +105,7 @@ def tile_moe_shr_lin_relu2_kernel(tc, xT, w, b, gate, offs, out):
                     gw[:, u, :, :].rearrange("p j e -> p (j e)").bitcast(U32),
                     xp[:, u, :, :].rearrange("p t e -> p (t e)").bitcast(U32).indirect(offsets[:]),
                 )
-            gi = xst1.tile([P, SLOTS, 2, 2], BF16, tag="gi", name=f"gi{c}", align_bytes=64)
+            gi = mixp.tile([P, SLOTS, 2, 2], BF16, tag="mix", name=f"gi{c}", align_bytes=64)
             nc.vector.tensor_copy(
                 gi[:].rearrange("p j u e -> p (j u e)").bitcast(I32).rearrange("p (j u) -> p j u", u=2),
                 gw[:].rearrange("p u j e -> p (u j e)").bitcast(I32).rearrange("p (u j) -> p j u", u=2),
@@ -103,17 +119,19 @@ def tile_moe_shr_lin_relu2_kernel(tc, xT, w, b, gate, offs, out):
             sq.append(scodes)
             ss.append(sscale)
 
-        load_w(2)
-        load_w(3)
+        load_through(3)
 
         xq, xs = [], []
 
         def quantise_tokens(c):
-            xi = xst1.tile([P, T, 2, 2], BF16, tag="xi", name=f"xi{c}", align_bytes=64)
-            nc.vector.tensor_copy(
-                xi[:].rearrange("p t u e -> p (t u e)").bitcast(I32).rearrange("p (t u) -> p t u", u=2),
-                xps[c][:].rearrange("p u t e -> p (u t e)").bitcast(I32).rearrange("p (u t) -> p t u", u=2),
-            )
+            xi = mixp.tile([P, T, 2, 2], BF16, tag="mix", name=f"xi{c}", align_bytes=64)
+            if c in SCALAR_TOKENS:
+                nc.scalar.copy(xi[:], xps[c][:].rearrange("p u t e -> p t u e"))
+            else:
+                nc.vector.tensor_copy(
+                    xi[:].rearrange("p t u e -> p (t u e)").bitcast(I32).rearrange("p (t u) -> p t u", u=2),
+                    xps[c][:].rearrange("p u t e -> p (u t e)").bitcast(I32).rearrange("p (u t) -> p t u", u=2),
+                )
             xcodes = keep.tile([P, T], U32, name=f"xcodes{c}", align_bytes=64)
             xscale = keep.tile([P, T], U8, name=f"xscale{c}", align_bytes=64)
             flat = xi[:].rearrange("p j u e -> p (j u e)")
@@ -131,16 +149,14 @@ def tile_moe_shr_lin_relu2_kernel(tc, xT, w, b, gate, offs, out):
             e, n0, n1 = columns(i)
             width = n1 - n0
             wb = wbfp.tile([P, PASSES, width, 4], BF16, tag="wb", name=f"wb{i}", align_bytes=64)
-            k1 = S_SHARE * width // N // 4
-            k2 = k1 + G_SHARE * width // N // 4
             for c in range(PASSES):
+                k = S_SHARE[i][c] * width // N // 4
                 dst = wb[:, c, :, :].rearrange("p (k i) t -> p k t i", i=4)
                 src = wr[e, c][:, :, n0:n1].rearrange("p t (k i) -> p k t i", i=4)
-                nc.scalar.copy(dst[:, 0:k1, :, :], src[:, 0:k1, :, :])
-                if k1 < k2:
-                    nc.gpsimd.tensor_scalar(dst[:, k1:k2, :, :], src[:, k1:k2, :, :], 1.0, 0.0, op0=ALU.mult, op1=ALU.add)
-                if k2 < width // 4:
-                    nc.vector.tensor_copy(dst[:, k2:, :, :], src[:, k2:, :, :])
+                if k > 0:
+                    nc.scalar.copy(dst[:, 0:k, :, :], src[:, 0:k, :, :])
+                if k < width // 4:
+                    nc.vector.tensor_copy(dst[:, k:, :, :], src[:, k:, :, :])
             cast_tiles[i] = wb
 
         def quantise(i):
@@ -188,6 +204,16 @@ def tile_moe_shr_lin_relu2_kernel(tc, xT, w, b, gate, offs, out):
                 if h == 0:
                     r[g] = rp.tile([P, NT, 2 * C], F32, tag="r", name=f"r{g}")
                 half = r[g][:, :, h * C : (h + 1) * C]
+                if EPILOGUE[i] != "S":
+                    nc.vector.tensor_tensor(
+                        half, banks[i][:], bias[:, :, i : i + 1].to_broadcast([P, NT, C]), ALU.add
+                    )
+                    if EPILOGUE[i] == "V":
+                        nc.vector.scalar_tensor_tensor(half, half, 0.0, half, op0=ALU.max, op1=ALU.mult)
+                    else:
+                        nc.scalar.activation(half, half, ACT.Relu)
+                        nc.scalar.activation(half, half, ACT.Square)
+                    return
                 for n in range(NT):
                     nc.scalar.activation(half[:, n, :], banks[i][:, n, :], ACT.Relu, bias=bias[:, n, i : i + 1])
                 nc.scalar.activation(half, half, ACT.Square)
@@ -201,32 +227,33 @@ def tile_moe_shr_lin_relu2_kernel(tc, xT, w, b, gate, offs, out):
                     )
                     if n == NT - 1:
                         nc.scalar.activation(yt[:, lo:hi], yt[:, lo:hi], ACT.Square)
-                if n < NT - 1:
+                if n in VECTOR_SQUARES:
+                    nc.vector.tensor_tensor(yt[:], yt[:], yt[:], ALU.mult)
+                elif n < NT - 1:
                     nc.scalar.activation(yt[:], yt[:], ACT.Square)
                 ys[n] = yt
 
-        def fill(items):
-            for g, n in items:
-                if g == "x":
-                    quantise_tokens(n)
-                    continue
+        def scatter(k):
+            for j in (2 * k, 2 * k + 1):
+                g, n = j // NT, j % NT
                 lo, hi = 2 * g * C, 2 * (g + 1) * C
                 nc.vector.tensor_tensor(
-                    z[n][:].indirect(offsets[:, lo // 16 : hi // 16]), r[g][:, n, :], gsb[:, lo:hi], ALU.mult
+                    z[n][:].indirect(offsets[:, lo // 16 : hi // 16]), r[g][:, n, :], gates[g, n][:], ALU.mult
                 )
 
         for i in range(E + 3):
-            if i + 4 <= E:
-                load_w(i + 4)
+            load_through(i + 4)
             if i < E + 2:
                 cast(i)
             if i > 0:
                 activate(i - 1)
-            fill(FILL.get(i, ()))
             if i < E + 2:
                 quantise(i)
                 multiply(i)
-            fill(POST.get(i, ()))
+            if i in (1, 2):
+                quantise_tokens(i - 1)
+            if i >= 3:
+                scatter(i - 3)
         for n in range(NT):
             for lo, hi in chunks if n == NT - 1 else ((0, T),):
                 nc.vector.tensor_tensor(ys[n][:, lo:hi], ys[n][:, lo:hi], z[n][:, lo:hi], ALU.add)

@@ -21,26 +21,29 @@ X4 = mybir.dt.float8_e4m3fn_x4
 ACT = mybir.ActivationFunctionType
 ALU = mybir.AluOpType
 
-S_SHARE = ((0, 512), (448, 480), (256, 256), (320, 0), (0, 512), (320, 512), (512, 0), (512, 416))
-EPILOGUE = "SSSSSS"
+S_SHARE = ((320, 416), (512, 0), (512, 0), (256, 512), (512, 0), (448, 512), (512, 480), (512, 512))
+EPILOGUE = "VSSSVS"
 VECTOR_SQUARES = ()
-SCALAR_TOKENS = (1, )
-X_VECTOR = (640, 800, 640, 0)
-GATES_AFTER = {(3, 1): [(0, 2)], (4, 0): [(0, 3)], (4, 1): [(0, 0)], (5, 0): [(1, 0), (1, 2), (1, 1), (1, 3)], (6, 0): [(2, 0)], (6, 1): [(0, 1), (2, 1), (2, 3), (2, 2)]}
+SCALAR_TOKENS = (0, )
+X_VECTOR = (640, 800, 0, 320)
+GATES_AFTER = {(3, 0): [(0, 2), (0, 0)], (3, 1): [(0, 3)], (4, 1): [(0, 1), (1, 3)], (6, 1): [(1, 0), (1, 1), (2, 0), (2, 2), (2, 1), (1, 2), (2, 3)]}
 
 
 def tile_moe_shr_lin_relu2_kernel(tc, xT, w, b, gate, offs, out):
     nc = tc.nc
     with ExitStack() as ctx:
         keep = ctx.enter_context(tc.tile_pool(name="keep", bufs=1))
-        raws = ctx.enter_context(tc.tile_pool(name="raws", bufs=8))
+        raws = ctx.enter_context(tc.tile_pool(name="raws", bufs=7))
         wbfp = ctx.enter_context(tc.tile_pool(name="wbfp", bufs=3))
         wqp = ctx.enter_context(tc.tile_pool(name="wqp", bufs=3))
         xst = ctx.enter_context(tc.tile_pool(name="xst", bufs=2))
         xst1 = ctx.enter_context(tc.tile_pool(name="xst1", bufs=1))
-        mixp = ctx.enter_context(tc.tile_pool(name="mixp", bufs=1))
+        mixp = ctx.enter_context(tc.tile_pool(name="mixp", bufs=2))
         rp = ctx.enter_context(tc.tile_pool(name="rp", bufs=3))
         psum = ctx.enter_context(tc.psum_pool(name="psum", bufs=8))
+
+        bias = keep.tile([P, NT, E + 1], F32, name="bias")
+        nc.scalar.dma_start(bias[:], b.rearrange("(n p) e -> p n e", p=P))
 
         offsets = keep.tile([P, SLOTS // 16], U16, name="offsets")
         nc.sync.dma_start(offsets[:], offs)
@@ -54,9 +57,6 @@ def tile_moe_shr_lin_relu2_kernel(tc, xT, w, b, gate, offs, out):
                 for lo, hi in zip(cuts[:-1], cuts[1:]):
                     nc.sync.dma_start(raw[:, :, lo:hi], rows[:, u, :, lo:hi])
                 xr[c, u] = raw
-
-        bias = keep.tile([P, NT, E + 1], F32, name="bias")
-        nc.sync.dma_start(bias[:], b.rearrange("(n p) e -> p n e", p=P))
 
         wr = {}
 

from contextlib import ExitStack

import concourse.mybir as mybir

K, T, E, C, N = 1024, 1280, 6, 128, 512
SLOTS = E * C
P = 128
KP = 512
PASSES = K // KP
NT = N // P

FLOPS = 2 * K * N * (SLOTS + T)

F32 = mybir.dt.float32
BF16 = mybir.dt.bfloat16
U32 = mybir.dt.uint32
I32 = mybir.dt.int32
U16 = mybir.dt.uint16
U8 = mybir.dt.uint8
X4 = mybir.dt.float8_e4m3fn_x4
ACT = mybir.ActivationFunctionType
ALU = mybir.AluOpType

S_SHARE = ((320, 416), (512, 0), (512, 0), (256, 512), (512, 0), (448, 512), (512, 480), (512, 512))
EPILOGUE = "VSSSVS"
VECTOR_SQUARES = ()
SCALAR_TOKENS = (0, )
X_VECTOR = (640, 800, 0, 320)
GATES_AFTER = {(3, 0): [(0, 2), (0, 0)], (3, 1): [(0, 3)], (4, 1): [(0, 1), (1, 3)], (6, 1): [(1, 0), (1, 1), (2, 0), (2, 2), (2, 1), (1, 2), (2, 3)]}


def tile_moe_shr_lin_relu2_kernel(tc, xT, w, b, gate, offs, out):
    nc = tc.nc
    with ExitStack() as ctx:
        keep = ctx.enter_context(tc.tile_pool(name="keep", bufs=1))
        raws = ctx.enter_context(tc.tile_pool(name="raws", bufs=7))
        wbfp = ctx.enter_context(tc.tile_pool(name="wbfp", bufs=3))
        wqp = ctx.enter_context(tc.tile_pool(name="wqp", bufs=3))
        xst = ctx.enter_context(tc.tile_pool(name="xst", bufs=2))
        xst1 = ctx.enter_context(tc.tile_pool(name="xst1", bufs=1))
        mixp = ctx.enter_context(tc.tile_pool(name="mixp", bufs=2))
        rp = ctx.enter_context(tc.tile_pool(name="rp", bufs=3))
        psum = ctx.enter_context(tc.psum_pool(name="psum", bufs=8))

        bias = keep.tile([P, NT, E + 1], F32, name="bias")
        nc.scalar.dma_start(bias[:], b.rearrange("(n p) e -> p n e", p=P))

        offsets = keep.tile([P, SLOTS // 16], U16, name="offsets")
        nc.sync.dma_start(offsets[:], offs)

        xr = {}
        for c in range(PASSES):
            rows = xT[c * KP : (c + 1) * KP, :].rearrange("(p u e) t -> p u e t", u=2, e=2)
            for u in range(2):
                raw = raws.tile([P, 2, T], F32, tag="raw", name=f"x{c}{u}")
                cuts = (0, T // 2, T) if (c, u) == (0, 0) else (0, T)
                for lo, hi in zip(cuts[:-1], cuts[1:]):
                    nc.sync.dma_start(raw[:, :, lo:hi], rows[:, u, :, lo:hi])
                xr[c, u] = raw

        wr = {}

        def load_w(e, c):
            raw = raws.tile([P, 4, N], F32, tag="raw", name=f"w{e}{c}")
            nc.sync.dma_start(raw[:], w[e, c * KP : (c + 1) * KP, :].rearrange("(p j) n -> p j n", j=4))
            wr[e, c] = raw

        order = []
        for e in range(E + 1):
            for c in range(PASSES):
                order.append((e, c))
                order.extend(("gate", piece) for piece in GATES_AFTER.get((e, c), ()))
        gates = {}

        def load_through(e):
            while order and (order[0][0] == "gate" or order[0][0] <= e):
                kind, what = order[0]
                order.remove(order[0])
                if kind == "gate":
                    g, n = what
                    piece = raws.tile([P, 2 * C], F32, tag="raw", name=f"gate{g}{n}")
                    nc.sync.dma_start(piece[:], gate[n * P : (n + 1) * P, 2 * g * C : 2 * (g + 1) * C])
                    gates[g, n] = piece
                else:
                    load_w(kind, what)

        load_through(1)

        z = []
        for n in range(NT):
            zt = keep.tile([P, T], F32, name=f"z{n}")
            nc.gpsimd.memset(zt[:], 0.0)
            z.append(zt)

        xps, sq, ss = [], [], []
        for c in range(PASSES):
            xp = xst.tile([P, 2, T, 2], BF16, tag="xp", name=f"xp{c}", align_bytes=64)
            gw = xst1.tile([P, 2, SLOTS, 2], BF16, tag="gw", name=f"gw{c}", align_bytes=64)
            for u in range(2):
                cut = T - X_VECTOR[2 * c + u]
                nc.scalar.copy(xp[:, u, 0:cut, :], xr[c, u][:, :, 0:cut].rearrange("p e t -> p t e"))
                if cut < T:
                    nc.vector.tensor_copy(xp[:, u, cut:T, :], xr[c, u][:, :, cut:T].rearrange("p e t -> p t e"))
                nc.vector.tensor_copy(
                    gw[:, u, :, :].rearrange("p j e -> p (j e)").bitcast(U32),
                    xp[:, u, :, :].rearrange("p t e -> p (t e)").bitcast(U32).indirect(offsets[:]),
                )
            gi = mixp.tile([P, SLOTS, 2, 2], BF16, tag="mix", name=f"gi{c}", align_bytes=64)
            nc.vector.tensor_copy(
                gi[:].rearrange("p j u e -> p (j u e)").bitcast(I32).rearrange("p (j u) -> p j u", u=2),
                gw[:].rearrange("p u j e -> p (u j e)").bitcast(I32).rearrange("p (u j) -> p j u", u=2),
            )
            scodes = keep.tile([P, SLOTS], U32, name=f"scodes{c}", align_bytes=64)
            sscale = keep.tile([P, SLOTS], U8, name=f"sscale{c}", align_bytes=64)
            flat = gi[:].rearrange("p j u e -> p (j u e)")
            for lo, hi in ((0, 512), (512, 768)):
                nc.vector.quantize_mx(scodes[:, lo:hi].bitcast(X4), sscale[:, lo:hi], flat[:, 4 * lo : 4 * hi])
            xps.append(xp)
            sq.append(scodes)
            ss.append(sscale)

        load_through(3)

        xq, xs = [], []

        def quantise_tokens(c):
            xi = mixp.tile([P, T, 2, 2], BF16, tag="mix", name=f"xi{c}", align_bytes=64)
            if c in SCALAR_TOKENS:
                nc.scalar.copy(xi[:], xps[c][:].rearrange("p u t e -> p t u e"))
            else:
                nc.vector.tensor_copy(
                    xi[:].rearrange("p t u e -> p (t u e)").bitcast(I32).rearrange("p (t u) -> p t u", u=2),
                    xps[c][:].rearrange("p u t e -> p (u t e)").bitcast(I32).rearrange("p (u t) -> p t u", u=2),
                )
            xcodes = keep.tile([P, T], U32, name=f"xcodes{c}", align_bytes=64)
            xscale = keep.tile([P, T], U8, name=f"xscale{c}", align_bytes=64)
            flat = xi[:].rearrange("p j u e -> p (j u e)")
            for lo, hi in ((0, 1024), (1024, 1280)):
                nc.vector.quantize_mx(xcodes[:, lo:hi].bitcast(X4), xscale[:, lo:hi], flat[:, 4 * lo : 4 * hi])
            xq.append(xcodes)
            xs.append(xscale)

        def columns(i):
            return (i, 0, N) if i < E else (E, (i - E) * N // 2, (i - E + 1) * N // 2)

        cast_tiles, weights, banks = {}, {}, {}

        def cast(i):
            e, n0, n1 = columns(i)
            width = n1 - n0
            wb = wbfp.tile([P, PASSES, width, 4], BF16, tag="wb", name=f"wb{i}", align_bytes=64)
            for c in range(PASSES):
                k = S_SHARE[i][c] * width // N // 4
                dst = wb[:, c, :, :].rearrange("p (k i) t -> p k t i", i=4)
                src = wr[e, c][:, :, n0:n1].rearrange("p t (k i) -> p k t i", i=4)
                if k > 0:
                    nc.scalar.copy(dst[:, 0:k, :, :], src[:, 0:k, :, :])
                if k < width // 4:
                    nc.vector.tensor_copy(dst[:, k:, :, :], src[:, k:, :, :])
            cast_tiles[i] = wb

        def quantise(i):
            e, n0, n1 = columns(i)
            width = n1 - n0
            q = wqp.tile([P, PASSES * width], U32, tag="wq", name=f"wq{i}", align_bytes=64)
            s = wqp.tile([P, PASSES * width], U8, tag="ws", name=f"ws{i}", align_bytes=64)
            nc.vector.quantize_mx(q[:].bitcast(X4), s[:], cast_tiles[i][:].rearrange("p c n t -> p (c n t)"))
            weights[i] = q, s, width

        def product(ps, i, m, codes, scales, lo, hi):
            q, s, width = weights[i]
            for c in range(PASSES):
                cols = slice(c * width + m * P, c * width + (m + 1) * P)
                nc.tensor.matmul_mx(
                    out=ps,
                    lhsT=q[:, cols].bitcast(X4),
                    lhsT_scale=s[:, cols],
                    rhs=codes[c][:, lo:hi].bitcast(X4),
                    rhs_scale=scales[c][:, lo:hi],
                    start=(c == 0),
                    stop=(c == PASSES - 1),
                )

        chunks = ((0, 512), (512, 1024), (1024, 1280))
        r, ys = {}, {}

        def multiply(i):
            if i < E:
                ps = psum.tile([P, NT, C], F32, tag="ps", name=f"ps{i}")
                for n in range(NT):
                    product(ps[:, n, :], i, n, sq, ss, i * C, (i + 1) * C)
                banks[i] = ps
                return
            for m in range(NT // 2):
                n = (i - E) * (NT // 2) + m
                for lo, hi in chunks:
                    ps = psum.tile([P, 512], F32, tag="ps", name=f"ps{i}_{n}_{lo}")
                    product(ps[:, 0 : hi - lo], i, m, xq, xs, lo, hi)
                    banks[n, lo] = ps

        def activate(i):
            if i < E:
                g, h = i // 2, i % 2
                if h == 0:
                    r[g] = rp.tile([P, NT, 2 * C], F32, tag="r", name=f"r{g}")
                half = r[g][:, :, h * C : (h + 1) * C]
                if EPILOGUE[i] != "S":
                    nc.vector.tensor_tensor(
                        half, banks[i][:], bias[:, :, i : i + 1].to_broadcast([P, NT, C]), ALU.add
                    )
                    if EPILOGUE[i] == "V":
                        nc.vector.scalar_tensor_tensor(half, half, 0.0, half, op0=ALU.max, op1=ALU.mult)
                    else:
                        nc.scalar.activation(half, half, ACT.Relu)
                        nc.scalar.activation(half, half, ACT.Square)
                    return
                for n in range(NT):
                    nc.scalar.activation(half[:, n, :], banks[i][:, n, :], ACT.Relu, bias=bias[:, n, i : i + 1])
                nc.scalar.activation(half, half, ACT.Square)
                return
            for m in range(NT // 2):
                n = (i - E) * (NT // 2) + m
                yt = keep.tile([P, T], F32, name=f"ys{n}")
                for lo, hi in chunks:
                    nc.scalar.activation(
                        yt[:, lo:hi], banks[n, lo][:, 0 : hi - lo], ACT.Relu, bias=bias[:, n, E : E + 1]
                    )
                    if n == NT - 1:
                        nc.scalar.activation(yt[:, lo:hi], yt[:, lo:hi], ACT.Square)
                if n in VECTOR_SQUARES:
                    nc.vector.tensor_tensor(yt[:], yt[:], yt[:], ALU.mult)
                elif n < NT - 1:
                    nc.scalar.activation(yt[:], yt[:], ACT.Square)
                ys[n] = yt

        def scatter(k):
            for j in (2 * k, 2 * k + 1):
                g, n = j // NT, j % NT
                lo, hi = 2 * g * C, 2 * (g + 1) * C
                nc.vector.tensor_tensor(
                    z[n][:].indirect(offsets[:, lo // 16 : hi // 16]), r[g][:, n, :], gates[g, n][:], ALU.mult
                )

        for i in range(E + 3):
            load_through(i + 4)
            if i < E + 2:
                cast(i)
            if i > 0:
                activate(i - 1)
            if i < E + 2:
                quantise(i)
                multiply(i)
            if i in (1, 2):
                quantise_tokens(i - 1)
            if i >= 3:
                scatter(i - 3)
        for n in range(NT):
            for lo, hi in chunks if n == NT - 1 else ((0, T),):
                nc.vector.tensor_tensor(ys[n][:, lo:hi], ys[n][:, lo:hi], z[n][:, lo:hi], ALU.add)
                nc.sync.dma_start(out[n * P : (n + 1) * P, lo:hi], ys[n][:, lo:hi])
